import numpy as np
import ml_dtypes


def mxq(x, axis, fmt="e4m3"):
    dtype, down = {"e4m3": (ml_dtypes.float8_e4m3fn, 7), "e5m2": (ml_dtypes.float8_e5m2, 14)}[fmt]
    v = np.moveaxis(np.asarray(x, np.float32).astype(ml_dtypes.bfloat16).astype(np.float64), axis, -1)
    blocks = v.reshape(v.shape[:-1] + (-1, 32))
    amax = np.abs(blocks).max(-1, keepdims=True)
    byte = np.maximum(np.where(amax > 0, np.frexp(amax)[1] - 1 + 127, 0) - down, 1)
    scale = np.exp2(byte - 127.0)
    codes = (blocks / scale).astype(np.float32).astype(dtype).astype(np.float64)
    return np.moveaxis((codes * scale).reshape(v.shape), -1, axis)


WIDE = False


def mx_kscale(k):
    if not WIDE:
        return np.ones(k)
    levels = np.array([30, -30])
    if k % 512:
        return np.exp2(np.random.permutation(np.resize(levels, k // 32))).repeat(32)
    a = np.empty((k // 512, 16))
    for p in range(k // 512):
        a[p, :8] = np.random.permutation(np.resize(levels, 8))
        for g in range(8):
            far = levels[np.abs(levels - a[p, g]) >= 10]
            a[p, g + 8] = far[np.random.randint(len(far))]
    return np.exp2(a.ravel()).repeat(32)


def f64(x):
    return np.asarray(x).astype(np.float64)


def striped(idx):
    return np.tile(np.asarray(idx).reshape(-1, 16).T, (8, 1)).astype(np.uint16)


def unstriped(offs):
    return offs[:16].T.reshape(-1).astype(np.int64)


E2M1 = np.array([0.0, 0.5, 1.0, 1.5, 2.0, 3.0, 4.0, 6.0, -0.0, -0.5, -1.0, -1.5, -2.0, -3.0, -4.0, -6.0])


def pack_weight(w, fmt):
    k, n = w.shape
    w = f64(np.asarray(w, np.float32).astype(ml_dtypes.bfloat16)).reshape(k // 32, 32, n)
    amax = np.abs(w).max(1)
    if fmt in ("e4m3", "e5m2"):
        byte = np.frexp(amax)[1] - 1 + 127 - (7 if fmt == "e4m3" else 14)
    else:
        mant, ex = np.frexp(amax / 6.0)
        byte = np.where(mant > 0.5, ex, ex - 1) + 127
    byte = np.clip(np.where(amax > 0, byte, 1), 1, 254)
    scaled = (w * np.exp2(127.0 - byte)[:, None, :]).reshape(k, n).astype(np.float32)
    by_word = np.ascontiguousarray(scaled.reshape(k // 512, 128, 4, n).transpose(0, 1, 3, 2))
    if fmt in ("e4m3", "e5m2"):
        words = by_word.astype(ml_dtypes.float8_e4m3fn if fmt == "e4m3" else ml_dtypes.float8_e5m2).view(np.uint8)
    else:
        c = by_word.astype(ml_dtypes.float4_e2m1fn).view(np.uint8) & 0xF
        words = (c[..., 0::2] | (c[..., 1::2] << 4)).reshape(k // 512, 128, 2 * n)
    return np.ascontiguousarray(words), np.ascontiguousarray(byte.astype(np.uint8).reshape(k // 512, 16, n))


def unpack_weight(words, scales, fmt):
    g, _, n = scales.shape
    words = np.ascontiguousarray(words).reshape(g, 128, n, -1)
    if fmt in ("e4m3", "e5m2"):
        vals = words.view(ml_dtypes.float8_e4m3fn if fmt == "e4m3" else ml_dtypes.float8_e5m2).astype(np.float64)
    else:
        nib = np.empty((g, 128, n, 4), np.uint8)
        nib[..., 0::2] = words & 0xF
        nib[..., 1::2] = words >> 4
        vals = E2M1[nib]
    vals = vals * np.repeat(np.exp2(scales.astype(np.float64) - 127.0), 8, axis=1)[..., None]
    return vals.transpose(0, 1, 3, 2).reshape(g * 512, n)


K, T, J, R, F, Z, C, X, O, N, U = 512, 1024, 256, 512, 512, 1024, 512, 1024, 256, 256, 128


def setup_inputs():
    n = np.random.standard_normal
    idx = np.random.permutation(T)[:J]
    idx2 = np.random.permutation(Z)[:J]
    idx3 = np.random.permutation(C)[:J]
    idx4 = np.random.permutation(X)[:C]
    idx5 = np.random.permutation(C)[:O]
    idx6 = np.random.permutation(O)[:U]
    idx7 = np.random.permutation(O)[:U]
    fk = mx_kscale(K)
    ff = mx_kscale(F)
    fr = mx_kscale(R)
    xtp = pack_weight(n((K, T)) / fk[:, None], "e5m2")
    xop = pack_weight(n((F, Z)) / ff[:, None], "e4m3")
    wp = pack_weight(n((K, R)) * 1 / np.sqrt(K) * fk[:, None] * fr, "e2m1")
    w0p = pack_weight(n((F, R)) * 1 / np.sqrt(F) * ff[:, None] * fr, "e2m1")
    wbp = pack_weight(n((R, N)) * 1 / np.sqrt(R) / fr[:, None], "e2m1")
    return {
        "xt_words": xtp[0],
        "xt_scales": xtp[1],
        "xo_words": xop[0],
        "xo_scales": xop[1],
        "w_words": wp[0],
        "w_scales": wp[1],
        "w0_words": w0p[0],
        "w0_scales": w0p[1],
        "tb": (n((R, X)) * 0.9).astype(np.float32),
        "wb_words": wbp[0],
        "wb_scales": wbp[1],
        "so": (np.random.uniform(0.5, 1.6, (N, 1))).astype(np.float32),
        "sp": (np.random.uniform(0.5, 1.6, (N, 1))).astype(np.float32),
        "offs": striped(idx),
        "offs2": striped(idx2),
        "offs3": striped(idx3),
        "offs4": striped(idx4),
        "offs5": striped(idx5),
        "offs6": striped(idx6),
        "offs7": striped(idx7),
    }


def reference(xt_words, xt_scales, xo_words, xo_scales, w_words, w_scales, w0_words, w0_scales, tb, wb_words, wb_scales, so, sp, offs, offs2, offs3, offs4, offs5, offs6, offs7):
    idx = unstriped(offs)
    idx2 = unstriped(offs2)
    idx3 = unstriped(offs3)
    idx4 = unstriped(offs4)
    idx5 = unstriped(offs5)
    idx6 = unstriped(offs6)
    idx7 = unstriped(offs7)
    xtu = unpack_weight(xt_words, xt_scales, "e5m2")
    xou = unpack_weight(xo_words, xo_scales, "e4m3")
    wu = unpack_weight(w_words, w_scales, "e2m1")
    w0u = unpack_weight(w0_words, w0_scales, "e2m1")
    wbu = unpack_weight(wb_words, wb_scales, "e2m1")
    xtidxg = xtu[:, idx]
    xoidx2g = xou[:, idx2]
    a = wu.T @ xtidxg + w0u.T @ xoidx2g
    la = a[:, 0:1]
    pw = np.zeros((R, C))
    pw[:, idx3] = a
    pg = np.abs(pw - f64(tb)[:, idx4] * la)
    hid = pg[:, idx5]
    hidq = mxq(hid, 0, "e4m3")
    p = wbu.T @ hidq
    y = np.maximum(p[:, idx6] * f64(so), p[:, idx7] * f64(sp))
    return y

@@ -1,0 +1,214 @@
+from contextlib import ExitStack
+
+import concourse.mybir as mybir
+
+K, T, J, R, F, Z, C, X, O, N, U = 512, 1024, 256, 512, 512, 1024, 512, 1024, 256, 256, 128
+FLOPS = 2 * (K * R * J + F * R * J + R * N * O)
+
+F32 = mybir.dt.float32
+BF16 = mybir.dt.bfloat16
+I32 = mybir.dt.int32
+U32 = mybir.dt.uint32
+U16 = mybir.dt.uint16
+U8 = mybir.dt.uint8
+E4M3 = mybir.dt.float8_e4m3fn_x4
+E5M2 = mybir.dt.float8_e5m2_x4
+E2M1 = mybir.dt.float4_e2m1fn_x4
+ALU = mybir.AluOpType
+ACT = mybir.ActivationFunctionType
+
+P = 128
+PACK = 4
+HALF = 64
+QUAD = 32
+
+
+def tile_list_stamplead_bank_one_pairweighed_kernel(
+    tc, xt_words, xt_scales, xo_words, xo_scales, w_words, w_scales, w0_words, w0_scales,
+    tb, wb_words, wb_scales, so, sp, offs, offs2, offs3, offs4, offs5, offs6, offs7, out,
+):
+    nc = tc.nc
+    with ExitStack() as ctx:
+        keep = ctx.enter_context(tc.tile_pool(name="keep", bufs=1))
+        psum = ctx.enter_context(tc.psum_pool(name="psum", bufs=1))
+
+        def sbuf(name, shape, dtype):
+            return keep.tile(shape, dtype, name=name, align_bytes=64)
+
+        def load_list(name, src):
+            tile = sbuf(name, list(src.shape), U16)
+            nc.sync.dma_start(tile[:], src)
+            return tile
+
+        def load_scale_halves(dst, scales):
+            rows = scales[0].bitcast(I32).rearrange("(h q r) n -> q r h n", h=2, q=2)
+            for q in range(2):
+                nc.sync.dma_start(dst[QUAD * q : QUAD * q + PACK], rows[q])
+
+        xt_stage = sbuf("xt_stage", [HALF, 2, T // 4], I32)
+        xo_stage = sbuf("xo_stage", [HALF, 2, Z // 4], I32)
+        w_stage = sbuf("w_stage", [P, 2, 2, R // 4], I32)
+        wb_plane = sbuf("wb_plane", [P, N], U8)
+        nc.vector.memset(xt_stage[:], 0)
+        nc.vector.memset(xo_stage[:], 0)
+        nc.vector.memset(w_stage[:], 0)
+        nc.vector.memset(wb_plane[:].bitcast(I32), 0)
+
+        load_scale_halves(xt_stage, xt_scales)
+        l1 = load_list("l1", offs)
+        load_scale_halves(xo_stage, xo_scales)
+        xt_w = sbuf("xt_w", [P, T], I32)
+        nc.sync.dma_start(xt_w[:], xt_words[0].rearrange("p c r -> p (c r)").bitcast(I32))
+        w_raw = sbuf("w_raw", [P, R], U16)
+        nc.sync.dma_start(w_raw[:].bitcast(I32), w_words[0].bitcast(I32))
+        w0_raw = sbuf("w0_raw", [P, R], U16)
+        nc.sync.dma_start(w0_raw[:].bitcast(I32), w0_words[0].bitcast(I32))
+        l2 = load_list("l2", offs2)
+        xo_w = sbuf("xo_w", [P, Z], I32)
+        nc.sync.dma_start(xo_w[:], xo_words[0].rearrange("p c r -> p (c r)").bitcast(I32))
+        load_scale_halves(w_stage[:, :, 0, :], w_scales)
+        load_scale_halves(w_stage[:, :, 1, :], w0_scales)
+        l4 = load_list("l4", offs4)
+        l3 = load_list("l3", offs3)
+        tb_rows = tb.rearrange("(p t) x -> t p x", t=PACK)
+        tb_s = []
+        for t in range(PACK):
+            tile = sbuf("tb%d" % t, [P, X], F32)
+            nc.sync.dma_start(tile[:], tb_rows[t])
+            tb_s.append(tile)
+        l5 = load_list("l5", offs5)
+        wb_w = sbuf("wb_w", [P, N], U16)
+        nc.sync.dma_start(wb_w[:].bitcast(I32), wb_words[0].bitcast(I32))
+        for q in range(4):
+            nc.sync.dma_start(
+                wb_plane[QUAD * q : QUAD * q + PACK, :].bitcast(I32),
+                wb_scales[0, PACK * q : PACK * q + PACK, :].bitcast(I32),
+            )
+        so_s = sbuf("so_s", [P, 2], F32)
+        sp_s = sbuf("sp_s", [P, 2], F32)
+        with nc.allow_non_contiguous_dma(reason="one weight a partition"):
+            nc.sync.dma_start(so_s[:], so.rearrange("(h p) o -> p (h o)", p=P))
+            nc.sync.dma_start(sp_s[:], sp.rearrange("(h p) o -> p (h o)", p=P))
+        l6 = load_list("l6", offs6)
+        l7 = load_list("l7", offs7)
+
+        pw = []
+        for t in range(PACK):
+            tile = sbuf("pw%d" % t, [P, C], F32)
+            nc.gpsimd.memset(tile[:], 0.0)
+            pw.append(tile)
+
+        w_d = sbuf("w_d", [P, PACK, P], U16)
+        w0_d = sbuf("w0_d", [P, PACK, P], U16)
+        nc.scalar.copy(w_d[:], w_raw[:].rearrange("p (m t) -> p t m", t=PACK))
+        nc.scalar.copy(w0_d[:], w0_raw[:].rearrange("p (m t) -> p t m", t=PACK))
+
+        xt_plane = sbuf("xt_plane", [P, T], U8)
+        xo_plane = sbuf("xo_plane", [P, Z], U8)
+        for plane, stage in ((xt_plane, xt_stage), (xo_plane, xo_stage)):
+            for h in range(2):
+                nc.vector.tensor_copy(plane[HALF * h : HALF * (h + 1), :].bitcast(I32), stage[:, h, :])
+        xt_gs = sbuf("xt_gs", [P, J], U8)
+        xt_gw = sbuf("xt_gw", [P, J], U32)
+        xo_gs = sbuf("xo_gs", [P, J], U8)
+        xo_gw = sbuf("xo_gw", [P, J], U32)
+        nc.vector.tensor_copy(xt_gs[:], xt_plane[:].indirect(l1[:]))
+        nc.vector.tensor_copy(xt_gw[:], xt_w[:].bitcast(U32).indirect(l1[:]))
+        nc.vector.tensor_copy(xo_gs[:], xo_plane[:].indirect(l2[:]))
+        nc.vector.tensor_copy(xo_gw[:], xo_w[:].bitcast(U32).indirect(l2[:]))
+        nc.vector.tensor_copy(w_stage[HALF:P, 0], w_stage[0:HALF, 1])
+        ws_d = sbuf("ws_d", [P, 2, PACK, P], U8)
+        nc.vector.tensor_copy(
+            ws_d[:], w_stage[:, 0].bitcast(U8).rearrange("p w (m t) -> p w t m", t=PACK)
+        )
+
+        a_ps = [psum.tile([P, J], F32, name="a_ps%d" % t) for t in range(PACK)]
+        for t in range(PACK):
+            nc.tensor.matmul_mx(
+                out=a_ps[t][:], lhsT=w_d[:, t, :].bitcast(E2M1), lhsT_scale=ws_d[:, 0, t, :],
+                rhs=xt_gw[:].bitcast(E5M2), rhs_scale=xt_gs[:], start=True, stop=False,
+            )
+            nc.tensor.matmul_mx(
+                out=a_ps[t][:], lhsT=w0_d[:, t, :].bitcast(E2M1), lhsT_scale=ws_d[:, 1, t, :],
+                rhs=xo_gw[:].bitcast(E4M3), rhs_scale=xo_gs[:], start=False, stop=True,
+            )
+
+        a_s = [sbuf("a%d" % t, [P, J], F32) for t in range(PACK)]
+        tl = [sbuf("tl%d" % t, [P, C], F32) for t in range(PACK)]
+        df = [sbuf("df%d" % t, [P, C], F32) for t in range(PACK)]
+        pg = [sbuf("pg%d" % t, [P, C], F32) for t in range(PACK)]
+        hid = sbuf("hid", [P, PACK, O], F32)
+
+        def evac(t):
+            if t == 0:
+                nc.vector.tensor_copy(a_s[t][:], a_ps[t][:])
+            else:
+                nc.scalar.copy(a_s[t][:], a_ps[t][:])
+
+        def scatter(t):
+            if t < PACK - 1:
+                nc.vector.tensor_copy(pw[t][:].indirect(l3[:]), a_s[t][:])
+            else:
+                nc.scalar.activation(pw[t][:].indirect(l3[:]), a_s[t][:], ACT.Copy)
+
+        def fetch(t):
+            nc.scalar.activation(tl[t][:], tb_s[t][:].indirect(l4[:]), ACT.Copy, scale=a_s[t][:, 0:1])
+
+        def diff(t):
+            nc.vector.tensor_tensor(df[t][:], pw[t][:], tl[t][:], ALU.subtract)
+
+        def magnitude(t):
+            nc.scalar.activation(pg[t][:], df[t][:], ACT.Abs)
+
+        def pick(t):
+            nc.vector.tensor_copy(hid[:, t, :], pg[t][:].indirect(l5[:]))
+
+        evac(0)
+        evac(1)
+        scatter(0)
+        fetch(0)
+        evac(2)
+        evac(3)
+        scatter(1)
+        fetch(1)
+        diff(0)
+        diff(1)
+        scatter(3)
+        scatter(2)
+        magnitude(0)
+        magnitude(1)
+        fetch(2)
+        pick(0)
+        pick(1)
+        fetch(3)
+        diff(2)
+        diff(3)
+        magnitude(2)
+        magnitude(3)
+        pick(2)
+        pick(3)
+
+        hb = sbuf("hb", [P, O, PACK], BF16)
+        nc.vector.tensor_copy(
+            hb[:].rearrange("p (c i) t -> p c t i", i=4), hid[:].rearrange("p t (c i) -> p c t i", i=4)
+        )
+        hq = sbuf("hq", [P, O], U32)
+        hs = sbuf("hs", [P, O], U8)
+        nc.vector.quantize_mx(out=hq[:].bitcast(E4M3), scales=hs[:], in_=hb[:].rearrange("p o t -> p (o t)"))
+
+        for h in range(2):
+            cols = slice(P * h, P * (h + 1))
+            p_ps = psum.tile([P, O], F32, name="p_ps%d" % h)
+            nc.tensor.matmul_mx(
+                out=p_ps[:], lhsT=wb_w[:, cols].bitcast(E2M1), lhsT_scale=wb_plane[:, cols],
+                rhs=hq[:].bitcast(E4M3), rhs_scale=hs[:], start=True, stop=True,
+            )
+            p_s = sbuf("p%d" % h, [P, O], F32)
+            nc.vector.tensor_copy(p_s[:], p_ps[:])
+            g6 = sbuf("g6_%d" % h, [P, U], F32)
+            g7 = sbuf("g7_%d" % h, [P, U], F32)
+            nc.scalar.activation(g6[:], p_s[:].indirect(l6[:]), ACT.Copy, scale=so_s[:, h : h + 1])
+            nc.scalar.activation(g7[:], p_s[:].indirect(l7[:]), ACT.Copy, scale=sp_s[:, h : h + 1])
+            y = sbuf("y%d" % h, [P, U], F32)
+            nc.vector.tensor_tensor(y[:], g6[:], g7[:], ALU.max)
+            nc.sync.dma_start(out[cols, :], y[:])

@@ -32,42 +32,44 @@ def tile_list_stamplead_bank_one_pairweighed_kernel(
         keep = ctx.enter_context(tc.tile_pool(name="keep", bufs=1))
         psum = ctx.enter_context(tc.psum_pool(name="psum", bufs=1))
 
-        def sbuf(name, shape, dtype):
-            return keep.tile(shape, dtype, name=name, align_bytes=64)
+        def sbuf(name, shape, dtype, tag=None):
+            return keep.tile(shape, dtype, name=name, tag=tag or name, align_bytes=64)
 
         def load_list(name, src):
             tile = sbuf(name, list(src.shape), U16)
             nc.sync.dma_start(tile[:], src)
             return tile
 
-        def load_scale_halves(dst, scales):
+        def load_scale_half(dst, scales, q):
             rows = scales[0].bitcast(I32).rearrange("(h q r) n -> q r h n", h=2, q=2)
-            for q in range(2):
-                nc.sync.dma_start(dst[QUAD * q : QUAD * q + PACK], rows[q])
+            nc.sync.dma_start(dst[QUAD * q : QUAD * q + PACK], rows[q])
 
         xt_stage = sbuf("xt_stage", [HALF, 2, T // 4], I32)
         xo_stage = sbuf("xo_stage", [HALF, 2, Z // 4], I32)
-        w_stage = sbuf("w_stage", [P, 2, 2, R // 4], I32)
+        w_stage = sbuf("w_stage", [PACK, PACK, 2, R // 4], I32)
+        w_plane = sbuf("w_plane", [P, 2, R // 4], I32)
         wb_plane = sbuf("wb_plane", [P, N], U8)
-        nc.vector.memset(xt_stage[:], 0)
-        nc.vector.memset(xo_stage[:], 0)
-        nc.vector.memset(w_stage[:], 0)
+        nc.gpsimd.memset(xt_stage[:], 0)
+        nc.vector.memset(w_plane[:], 0)
+        nc.gpsimd.memset(xo_stage[:], 0)
         nc.vector.memset(wb_plane[:].bitcast(I32), 0)
 
-        load_scale_halves(xt_stage, xt_scales)
+        for i, scales in enumerate((w_scales, w0_scales)):
+            nc.sync.dma_start(w_stage[:, :, i, :], scales[0].bitcast(I32).rearrange("(q r) n -> r q n", r=PACK))
+        for q in range(2):
+            load_scale_half(xt_stage, xt_scales, q)
         l1 = load_list("l1", offs)
-        load_scale_halves(xo_stage, xo_scales)
-        xt_w = sbuf("xt_w", [P, T], I32)
-        nc.sync.dma_start(xt_w[:], xt_words[0].rearrange("p c r -> p (c r)").bitcast(I32))
         w_raw = sbuf("w_raw", [P, R], U16)
         nc.sync.dma_start(w_raw[:].bitcast(I32), w_words[0].bitcast(I32))
+        load_scale_half(xo_stage, xo_scales, 0)
+        xt_w = sbuf("xt_w", [P, T], I32)
+        nc.sync.dma_start(xt_w[:], xt_words[0].rearrange("p c r -> p (c r)").bitcast(I32))
+        load_scale_half(xo_stage, xo_scales, 1)
+        l2 = load_list("l2", offs2)
         w0_raw = sbuf("w0_raw", [P, R], U16)
         nc.sync.dma_start(w0_raw[:].bitcast(I32), w0_words[0].bitcast(I32))
-        l2 = load_list("l2", offs2)
         xo_w = sbuf("xo_w", [P, Z], I32)
         nc.sync.dma_start(xo_w[:], xo_words[0].rearrange("p c r -> p (c r)").bitcast(I32))
-        load_scale_halves(w_stage[:, :, 0, :], w_scales)
-        load_scale_halves(w_stage[:, :, 1, :], w0_scales)
         l4 = load_list("l4", offs4)
         l3 = load_list("l3", offs3)
         tb_rows = tb.rearrange("(p t) x -> t p x", t=PACK)
@@ -99,28 +101,34 @@ def tile_list_stamplead_bank_one_pairweighed_kernel(
             pw.append(tile)
 
         w_d = sbuf("w_d", [P, PACK, P], U16)
-        w0_d = sbuf("w0_d", [P, PACK, P], U16)
+        w0_d = [sbuf("w0_d%d" % t, [P, P], U16) for t in range(PACK)]
         nc.scalar.copy(w_d[:], w_raw[:].rearrange("p (m t) -> p t m", t=PACK))
-        nc.scalar.copy(w0_d[:], w0_raw[:].rearrange("p (m t) -> p t m", t=PACK))
+        for t in range(PACK):
+            nc.scalar.copy(w0_d[t][:], w0_raw[:, t::PACK])
 
         xt_plane = sbuf("xt_plane", [P, T], U8)
         xo_plane = sbuf("xo_plane", [P, Z], U8)
-        for plane, stage in ((xt_plane, xt_stage), (xo_plane, xo_stage)):
-            for h in range(2):
-                nc.vector.tensor_copy(plane[HALF * h : HALF * (h + 1), :].bitcast(I32), stage[:, h, :])
         xt_gs = sbuf("xt_gs", [P, J], U8)
         xt_gw = sbuf("xt_gw", [P, J], U32)
         xo_gs = sbuf("xo_gs", [P, J], U8)
         xo_gw = sbuf("xo_gw", [P, J], U32)
+        ws_d = sbuf("ws_d", [P, 2, PACK, P], U8)
+
+        def spread(plane, stage):
+            for h in range(2):
+                nc.vector.tensor_copy(plane[HALF * h : HALF * (h + 1), :].bitcast(I32), stage[:, h, :])
+
+        for q in range(PACK):
+            nc.vector.tensor_copy(w_plane[QUAD * q : QUAD * q + PACK], w_stage[:, q])
+        nc.gpsimd.tensor_copy(
+            ws_d[:], w_plane[:].bitcast(U8).rearrange("p w (m t) -> p w t m", t=PACK)
+        )
+        spread(xt_plane, xt_stage)
         nc.vector.tensor_copy(xt_gs[:], xt_plane[:].indirect(l1[:]))
         nc.vector.tensor_copy(xt_gw[:], xt_w[:].bitcast(U32).indirect(l1[:]))
+        spread(xo_plane, xo_stage)
         nc.vector.tensor_copy(xo_gs[:], xo_plane[:].indirect(l2[:]))
         nc.vector.tensor_copy(xo_gw[:], xo_w[:].bitcast(U32).indirect(l2[:]))
-        nc.vector.tensor_copy(w_stage[HALF:P, 0], w_stage[0:HALF, 1])
-        ws_d = sbuf("ws_d", [P, 2, PACK, P], U8)
-        nc.vector.tensor_copy(
-            ws_d[:], w_stage[:, 0].bitcast(U8).rearrange("p w (m t) -> p w t m", t=PACK)
-        )
 
         a_ps = [psum.tile([P, J], F32, name="a_ps%d" % t) for t in range(PACK)]
         for t in range(PACK):
@@ -128,83 +136,61 @@ def tile_list_stamplead_bank_one_pairweighed_kernel(
                 out=a_ps[t][:], lhsT=w_d[:, t, :].bitcast(E2M1), lhsT_scale=ws_d[:, 0, t, :],
                 rhs=xt_gw[:].bitcast(E5M2), rhs_scale=xt_gs[:], start=True, stop=False,
             )
+        for t in range(PACK):
             nc.tensor.matmul_mx(
-                out=a_ps[t][:], lhsT=w0_d[:, t, :].bitcast(E2M1), lhsT_scale=ws_d[:, 1, t, :],
+                out=a_ps[t][:], lhsT=w0_d[t][:].bitcast(E2M1), lhsT_scale=ws_d[:, 1, t, :],
                 rhs=xo_gw[:].bitcast(E4M3), rhs_scale=xo_gs[:], start=False, stop=True,
             )
 
         a_s = [sbuf("a%d" % t, [P, J], F32) for t in range(PACK)]
         tl = [sbuf("tl%d" % t, [P, C], F32) for t in range(PACK)]
         df = [sbuf("df%d" % t, [P, C], F32) for t in range(PACK)]
-        pg = [sbuf("pg%d" % t, [P, C], F32) for t in range(PACK)]
+        last = PACK - 1
+        pg_early = sbuf("pg_early", [P, last, C], F32, tag="tb%d" % last)
+        pg_last = sbuf("pg_last", [P, C], F32)
+        pg = [pg_early[:, t, :] for t in range(last)] + [pg_last[:]]
         hid = sbuf("hid", [P, PACK, O], F32)
 
-        def evac(t):
-            if t == 0:
-                nc.vector.tensor_copy(a_s[t][:], a_ps[t][:])
-            else:
-                nc.scalar.copy(a_s[t][:], a_ps[t][:])
-
-        def scatter(t):
-            if t < PACK - 1:
-                nc.vector.tensor_copy(pw[t][:].indirect(l3[:]), a_s[t][:])
-            else:
-                nc.scalar.activation(pw[t][:].indirect(l3[:]), a_s[t][:], ACT.Copy)
-
-        def fetch(t):
+        nc.vector.tensor_copy(a_s[0][:], a_ps[0][:])
+        for t in range(1, PACK):
+            nc.scalar.copy(a_s[t][:], a_ps[t][:])
+        for t in range(PACK):
+            nc.vector.tensor_copy(pw[t][:].indirect(l3[:]), a_s[t][:])
             nc.scalar.activation(tl[t][:], tb_s[t][:].indirect(l4[:]), ACT.Copy, scale=a_s[t][:, 0:1])
-
-        def diff(t):
-            nc.vector.tensor_tensor(df[t][:], pw[t][:], tl[t][:], ALU.subtract)
-
-        def magnitude(t):
-            nc.scalar.activation(pg[t][:], df[t][:], ACT.Abs)
-
-        def pick(t):
-            nc.vector.tensor_copy(hid[:, t, :], pg[t][:].indirect(l5[:]))
-
-        evac(0)
-        evac(1)
-        scatter(0)
-        fetch(0)
-        evac(2)
-        evac(3)
-        scatter(1)
-        fetch(1)
-        diff(0)
-        diff(1)
-        scatter(3)
-        scatter(2)
-        magnitude(0)
-        magnitude(1)
-        fetch(2)
-        pick(0)
-        pick(1)
-        fetch(3)
-        diff(2)
-        diff(3)
-        magnitude(2)
-        magnitude(3)
-        pick(2)
-        pick(3)
+            engine = nc.gpsimd if t < last else nc.vector
+            engine.tensor_tensor(df[t][:], pw[t][:], tl[t][:], ALU.subtract)
+        for t in range(PACK):
+            nc.scalar.activation(pg[t], df[t][:], ACT.Abs)
+        for t in range(2):
+            nc.vector.tensor_copy(hid[:, t, :], pg[t].indirect(l5[:]))
+        nc.scalar.activation(hid[:, 2, :], pg[2].indirect(l5[:]), ACT.Copy)
 
         hb = sbuf("hb", [P, O, PACK], BF16)
-        nc.vector.tensor_copy(
-            hb[:].rearrange("p (c i) t -> p c t i", i=4), hid[:].rearrange("p t (c i) -> p c t i", i=4)
-        )
         hq = sbuf("hq", [P, O], U32)
         hs = sbuf("hs", [P, O], U8)
-        nc.vector.quantize_mx(out=hq[:].bitcast(E4M3), scales=hs[:], in_=hb[:].rearrange("p o t -> p (o t)"))
+        halves = [slice(0, O // 2), slice(O // 2, O)]
+        nc.vector.tensor_copy(hid[:, last, halves[0]], pg[last].indirect(l5[:, 0:8]))
+        nc.scalar.activation(hid[:, last, halves[1]], pg[last].indirect(l5[:, 8:16]), ACT.Copy)
+        for half in halves:
+            nc.vector.tensor_copy(
+                hb[:, half, :].rearrange("p (c i) t -> p c t i", i=4),
+                hid[:, :, half].rearrange("p t (c i) -> p c t i", i=4),
+            )
+        for half in halves:
+            nc.vector.quantize_mx(
+                out=hq[:, half].bitcast(E4M3), scales=hs[:, half], in_=hb[:, half, :].rearrange("p o t -> p (o t)")
+            )
 
         for h in range(2):
             cols = slice(P * h, P * (h + 1))
-            p_ps = psum.tile([P, O], F32, name="p_ps%d" % h)
-            nc.tensor.matmul_mx(
-                out=p_ps[:], lhsT=wb_w[:, cols].bitcast(E2M1), lhsT_scale=wb_plane[:, cols],
-                rhs=hq[:].bitcast(E4M3), rhs_scale=hs[:], start=True, stop=True,
-            )
             p_s = sbuf("p%d" % h, [P, O], F32)
-            nc.vector.tensor_copy(p_s[:], p_ps[:])
+            for i, part in enumerate(halves if h == 0 else [slice(0, O)]):
+                p_ps = psum.tile([P, part.stop - part.start], F32, name="p_ps%d_%d" % (h, i))
+                nc.tensor.matmul_mx(
+                    out=p_ps[:], lhsT=wb_w[:, cols].bitcast(E2M1), lhsT_scale=wb_plane[:, cols],
+                    rhs=hq[:, part].bitcast(E4M3), rhs_scale=hs[:, part], start=True, stop=True,
+                )
+                nc.vector.tensor_copy(p_s[:, part], p_ps[:])
             g6 = sbuf("g6_%d" % h, [P, U], F32)
             g7 = sbuf("g7_%d" % h, [P, U], F32)
             nc.scalar.activation(g6[:], p_s[:].indirect(l6[:]), ACT.Copy, scale=so_s[:, h : h + 1])

@@ -49,22 +49,25 @@ def tile_list_stamplead_bank_one_pairweighed_kernel(
         w_stage = sbuf("w_stage", [PACK, PACK, 2, R // 4], I32)
         w_plane = sbuf("w_plane", [P, 2, R // 4], I32)
         wb_plane = sbuf("wb_plane", [P, N], U8)
-        nc.gpsimd.memset(xt_stage[:], 0)
-        nc.vector.memset(w_plane[:], 0)
+        nc.vector.memset(xt_stage[:], 0)
         nc.gpsimd.memset(xo_stage[:], 0)
+        nc.vector.memset(w_plane[:], 0)
         nc.vector.memset(wb_plane[:].bitcast(I32), 0)
 
-        for i, scales in enumerate((w_scales, w0_scales)):
+        def load_scale_rows(i, scales):
             nc.sync.dma_start(w_stage[:, :, i, :], scales[0].bitcast(I32).rearrange("(q r) n -> r q n", r=PACK))
+
+        load_scale_rows(0, w_scales)
+        load_scale_rows(1, w0_scales)
         for q in range(2):
             load_scale_half(xt_stage, xt_scales, q)
+        for q in range(2):
+            load_scale_half(xo_stage, xo_scales, q)
         l1 = load_list("l1", offs)
-        w_raw = sbuf("w_raw", [P, R], U16)
-        nc.sync.dma_start(w_raw[:].bitcast(I32), w_words[0].bitcast(I32))
-        load_scale_half(xo_stage, xo_scales, 0)
         xt_w = sbuf("xt_w", [P, T], I32)
         nc.sync.dma_start(xt_w[:], xt_words[0].rearrange("p c r -> p (c r)").bitcast(I32))
-        load_scale_half(xo_stage, xo_scales, 1)
+        w_raw = sbuf("w_raw", [P, R], U16)
+        nc.sync.dma_start(w_raw[:].bitcast(I32), w_words[0].bitcast(I32))
         l2 = load_list("l2", offs2)
         w0_raw = sbuf("w0_raw", [P, R], U16)
         nc.sync.dma_start(w0_raw[:].bitcast(I32), w0_words[0].bitcast(I32))
@@ -95,10 +98,11 @@ def tile_list_stamplead_bank_one_pairweighed_kernel(
         l7 = load_list("l7", offs7)
 
         pw = []
-        for t in range(PACK):
+        for t in range(PACK - 1):
             tile = sbuf("pw%d" % t, [P, C], F32)
-            nc.gpsimd.memset(tile[:], 0.0)
+            nc.vector.memset(tile[:], 0.0)
             pw.append(tile)
+        pw.append(pw[0])
 
         w_d = sbuf("w_d", [P, PACK, P], U16)
         w0_d = [sbuf("w0_d%d" % t, [P, P], U16) for t in range(PACK)]
@@ -112,7 +116,7 @@ def tile_list_stamplead_bank_one_pairweighed_kernel(
         xt_gw = sbuf("xt_gw", [P, J], U32)
         xo_gs = sbuf("xo_gs", [P, J], U8)
         xo_gw = sbuf("xo_gw", [P, J], U32)
-        ws_d = sbuf("ws_d", [P, 2, PACK, P], U8)
+        ws_d = sbuf("ws_d", [P, 2, PACK, P], U8, tag="xo_stage")
 
         def spread(plane, stage):
             for h in range(2):
@@ -120,13 +124,14 @@ def tile_list_stamplead_bank_one_pairweighed_kernel(
 
         for q in range(PACK):
             nc.vector.tensor_copy(w_plane[QUAD * q : QUAD * q + PACK], w_stage[:, q])
-        nc.gpsimd.tensor_copy(
-            ws_d[:], w_plane[:].bitcast(U8).rearrange("p w (m t) -> p w t m", t=PACK)
-        )
         spread(xt_plane, xt_stage)
+        spread(xo_plane, xo_stage)
+        for i in range(2):
+            nc.gpsimd.tensor_copy(
+                ws_d[:, i], w_plane[:, i, :].bitcast(U8).rearrange("p (m t) -> p t m", t=PACK)
+            )
         nc.vector.tensor_copy(xt_gs[:], xt_plane[:].indirect(l1[:]))
         nc.vector.tensor_copy(xt_gw[:], xt_w[:].bitcast(U32).indirect(l1[:]))
-        spread(xo_plane, xo_stage)
         nc.vector.tensor_copy(xo_gs[:], xo_plane[:].indirect(l2[:]))
         nc.vector.tensor_copy(xo_gw[:], xo_w[:].bitcast(U32).indirect(l2[:]))
 

from contextlib import ExitStack

import concourse.mybir as mybir

K, T, J, R, F, Z, C, X, O, N, U = 512, 1024, 256, 512, 512, 1024, 512, 1024, 256, 256, 128
FLOPS = 2 * (K * R * J + F * R * J + R * N * O)

F32 = mybir.dt.float32
BF16 = mybir.dt.bfloat16
I32 = mybir.dt.int32
U32 = mybir.dt.uint32
U16 = mybir.dt.uint16
U8 = mybir.dt.uint8
E4M3 = mybir.dt.float8_e4m3fn_x4
E5M2 = mybir.dt.float8_e5m2_x4
E2M1 = mybir.dt.float4_e2m1fn_x4
ALU = mybir.AluOpType
ACT = mybir.ActivationFunctionType

P = 128
PACK = 4
HALF = 64
QUAD = 32


def tile_list_stamplead_bank_one_pairweighed_kernel(
    tc, xt_words, xt_scales, xo_words, xo_scales, w_words, w_scales, w0_words, w0_scales,
    tb, wb_words, wb_scales, so, sp, offs, offs2, offs3, offs4, offs5, offs6, offs7, out,
):
    nc = tc.nc
    with ExitStack() as ctx:
        keep = ctx.enter_context(tc.tile_pool(name="keep", bufs=1))
        psum = ctx.enter_context(tc.psum_pool(name="psum", bufs=1))

        def sbuf(name, shape, dtype, tag=None):
            return keep.tile(shape, dtype, name=name, tag=tag or name, align_bytes=64)

        def load_list(name, src):
            tile = sbuf(name, list(src.shape), U16)
            nc.sync.dma_start(tile[:], src)
            return tile

        def load_scale_half(dst, scales, q):
            rows = scales[0].bitcast(I32).rearrange("(h q r) n -> q r h n", h=2, q=2)
            nc.sync.dma_start(dst[QUAD * q : QUAD * q + PACK], rows[q])

        xt_stage = sbuf("xt_stage", [HALF, 2, T // 4], I32)
        xo_stage = sbuf("xo_stage", [HALF, 2, Z // 4], I32)
        w_stage = sbuf("w_stage", [PACK, PACK, 2, R // 4], I32)
        w_plane = sbuf("w_plane", [P, 2, R // 4], I32)
        wb_plane = sbuf("wb_plane", [P, N], U8)
        nc.vector.memset(xt_stage[:], 0)
        nc.gpsimd.memset(xo_stage[:], 0)
        nc.vector.memset(w_plane[:], 0)
        nc.vector.memset(wb_plane[:].bitcast(I32), 0)

        def load_scale_rows(i, scales):
            nc.sync.dma_start(w_stage[:, :, i, :], scales[0].bitcast(I32).rearrange("(q r) n -> r q n", r=PACK))

        load_scale_rows(0, w_scales)
        load_scale_rows(1, w0_scales)
        for q in range(2):
            load_scale_half(xt_stage, xt_scales, q)
        for q in range(2):
            load_scale_half(xo_stage, xo_scales, q)
        l1 = load_list("l1", offs)
        xt_w = sbuf("xt_w", [P, T], I32)
        nc.sync.dma_start(xt_w[:], xt_words[0].rearrange("p c r -> p (c r)").bitcast(I32))
        w_raw = sbuf("w_raw", [P, R], U16)
        nc.sync.dma_start(w_raw[:].bitcast(I32), w_words[0].bitcast(I32))
        l2 = load_list("l2", offs2)
        w0_raw = sbuf("w0_raw", [P, R], U16)
        nc.sync.dma_start(w0_raw[:].bitcast(I32), w0_words[0].bitcast(I32))
        xo_w = sbuf("xo_w", [P, Z], I32)
        nc.sync.dma_start(xo_w[:], xo_words[0].rearrange("p c r -> p (c r)").bitcast(I32))
        l4 = load_list("l4", offs4)
        l3 = load_list("l3", offs3)
        tb_rows = tb.rearrange("(p t) x -> t p x", t=PACK)
        tb_s = []
        for t in range(PACK):
            tile = sbuf("tb%d" % t, [P, X], F32)
            nc.sync.dma_start(tile[:], tb_rows[t])
            tb_s.append(tile)
        l5 = load_list("l5", offs5)
        wb_w = sbuf("wb_w", [P, N], U16)
        nc.sync.dma_start(wb_w[:].bitcast(I32), wb_words[0].bitcast(I32))
        for q in range(4):
            nc.sync.dma_start(
                wb_plane[QUAD * q : QUAD * q + PACK, :].bitcast(I32),
                wb_scales[0, PACK * q : PACK * q + PACK, :].bitcast(I32),
            )
        so_s = sbuf("so_s", [P, 2], F32)
        sp_s = sbuf("sp_s", [P, 2], F32)
        with nc.allow_non_contiguous_dma(reason="one weight a partition"):
            nc.sync.dma_start(so_s[:], so.rearrange("(h p) o -> p (h o)", p=P))
            nc.sync.dma_start(sp_s[:], sp.rearrange("(h p) o -> p (h o)", p=P))
        l6 = load_list("l6", offs6)
        l7 = load_list("l7", offs7)

        pw = []
        for t in range(PACK - 1):
            tile = sbuf("pw%d" % t, [P, C], F32)
            nc.vector.memset(tile[:], 0.0)
            pw.append(tile)
        pw.append(pw[0])

        w_d = sbuf("w_d", [P, PACK, P], U16)
        w0_d = [sbuf("w0_d%d" % t, [P, P], U16) for t in range(PACK)]
        nc.scalar.copy(w_d[:], w_raw[:].rearrange("p (m t) -> p t m", t=PACK))
        for t in range(PACK):
            nc.scalar.copy(w0_d[t][:], w0_raw[:, t::PACK])

        xt_plane = sbuf("xt_plane", [P, T], U8)
        xo_plane = sbuf("xo_plane", [P, Z], U8)
        xt_gs = sbuf("xt_gs", [P, J], U8)
        xt_gw = sbuf("xt_gw", [P, J], U32)
        xo_gs = sbuf("xo_gs", [P, J], U8)
        xo_gw = sbuf("xo_gw", [P, J], U32)
        ws_d = sbuf("ws_d", [P, 2, PACK, P], U8, tag="xo_stage")

        def spread(plane, stage):
            for h in range(2):
                nc.vector.tensor_copy(plane[HALF * h : HALF * (h + 1), :].bitcast(I32), stage[:, h, :])

        for q in range(PACK):
            nc.vector.tensor_copy(w_plane[QUAD * q : QUAD * q + PACK], w_stage[:, q])
        spread(xt_plane, xt_stage)
        spread(xo_plane, xo_stage)
        for i in range(2):
            nc.gpsimd.tensor_copy(
                ws_d[:, i], w_plane[:, i, :].bitcast(U8).rearrange("p (m t) -> p t m", t=PACK)
            )
        nc.vector.tensor_copy(xt_gs[:], xt_plane[:].indirect(l1[:]))
        nc.vector.tensor_copy(xt_gw[:], xt_w[:].bitcast(U32).indirect(l1[:]))
        nc.vector.tensor_copy(xo_gs[:], xo_plane[:].indirect(l2[:]))
        nc.vector.tensor_copy(xo_gw[:], xo_w[:].bitcast(U32).indirect(l2[:]))

        a_ps = [psum.tile([P, J], F32, name="a_ps%d" % t) for t in range(PACK)]
        for t in range(PACK):
            nc.tensor.matmul_mx(
                out=a_ps[t][:], lhsT=w_d[:, t, :].bitcast(E2M1), lhsT_scale=ws_d[:, 0, t, :],
                rhs=xt_gw[:].bitcast(E5M2), rhs_scale=xt_gs[:], start=True, stop=False,
            )
        for t in range(PACK):
            nc.tensor.matmul_mx(
                out=a_ps[t][:], lhsT=w0_d[t][:].bitcast(E2M1), lhsT_scale=ws_d[:, 1, t, :],
                rhs=xo_gw[:].bitcast(E4M3), rhs_scale=xo_gs[:], start=False, stop=True,
            )

        a_s = [sbuf("a%d" % t, [P, J], F32) for t in range(PACK)]
        tl = [sbuf("tl%d" % t, [P, C], F32) for t in range(PACK)]
        df = [sbuf("df%d" % t, [P, C], F32) for t in range(PACK)]
        last = PACK - 1
        pg_early = sbuf("pg_early", [P, last, C], F32, tag="tb%d" % last)
        pg_last = sbuf("pg_last", [P, C], F32)
        pg = [pg_early[:, t, :] for t in range(last)] + [pg_last[:]]
        hid = sbuf("hid", [P, PACK, O], F32)

        nc.vector.tensor_copy(a_s[0][:], a_ps[0][:])
        for t in range(1, PACK):
            nc.scalar.copy(a_s[t][:], a_ps[t][:])
        for t in range(PACK):
            nc.vector.tensor_copy(pw[t][:].indirect(l3[:]), a_s[t][:])
            nc.scalar.activation(tl[t][:], tb_s[t][:].indirect(l4[:]), ACT.Copy, scale=a_s[t][:, 0:1])
            engine = nc.gpsimd if t < last else nc.vector
            engine.tensor_tensor(df[t][:], pw[t][:], tl[t][:], ALU.subtract)
        for t in range(PACK):
            nc.scalar.activation(pg[t], df[t][:], ACT.Abs)
        for t in range(2):
            nc.vector.tensor_copy(hid[:, t, :], pg[t].indirect(l5[:]))
        nc.scalar.activation(hid[:, 2, :], pg[2].indirect(l5[:]), ACT.Copy)

        hb = sbuf("hb", [P, O, PACK], BF16)
        hq = sbuf("hq", [P, O], U32)
        hs = sbuf("hs", [P, O], U8)
        halves = [slice(0, O // 2), slice(O // 2, O)]
        nc.vector.tensor_copy(hid[:, last, halves[0]], pg[last].indirect(l5[:, 0:8]))
        nc.scalar.activation(hid[:, last, halves[1]], pg[last].indirect(l5[:, 8:16]), ACT.Copy)
        for half in halves:
            nc.vector.tensor_copy(
                hb[:, half, :].rearrange("p (c i) t -> p c t i", i=4),
                hid[:, :, half].rearrange("p t (c i) -> p c t i", i=4),
            )
        for half in halves:
            nc.vector.quantize_mx(
                out=hq[:, half].bitcast(E4M3), scales=hs[:, half], in_=hb[:, half, :].rearrange("p o t -> p (o t)")
            )

        for h in range(2):
            cols = slice(P * h, P * (h + 1))
            p_s = sbuf("p%d" % h, [P, O], F32)
            for i, part in enumerate(halves if h == 0 else [slice(0, O)]):
                p_ps = psum.tile([P, part.stop - part.start], F32, name="p_ps%d_%d" % (h, i))
                nc.tensor.matmul_mx(
                    out=p_ps[:], lhsT=wb_w[:, cols].bitcast(E2M1), lhsT_scale=wb_plane[:, cols],
                    rhs=hq[:, part].bitcast(E4M3), rhs_scale=hs[:, part], start=True, stop=True,
                )
                nc.vector.tensor_copy(p_s[:, part], p_ps[:])
            g6 = sbuf("g6_%d" % h, [P, U], F32)
            g7 = sbuf("g7_%d" % h, [P, U], F32)
            nc.scalar.activation(g6[:], p_s[:].indirect(l6[:]), ACT.Copy, scale=so_s[:, h : h + 1])
            nc.scalar.activation(g7[:], p_s[:].indirect(l7[:]), ACT.Copy, scale=sp_s[:, h : h + 1])
            y = sbuf("y%d" % h, [P, U], F32)
            nc.vector.tensor_tensor(y[:], g6[:], g7[:], ALU.max)
            nc.sync.dma_start(out[cols, :], y[:])
